import numpy as np
import ml_dtypes


def mxq(x, axis, fmt="e4m3"):
    dtype, down = {"e4m3": (ml_dtypes.float8_e4m3fn, 7), "e5m2": (ml_dtypes.float8_e5m2, 14)}[fmt]
    v = np.moveaxis(np.asarray(x, np.float32).astype(ml_dtypes.bfloat16).astype(np.float64), axis, -1)
    blocks = v.reshape(v.shape[:-1] + (-1, 32))
    amax = np.abs(blocks).max(-1, keepdims=True)
    byte = np.maximum(np.where(amax > 0, np.frexp(amax)[1] - 1 + 127, 0) - down, 1)
    scale = np.exp2(byte - 127.0)
    codes = (blocks / scale).astype(np.float32).astype(dtype).astype(np.float64)
    return np.moveaxis((codes * scale).reshape(v.shape), -1, axis)


WIDE = False


def mx_kscale(k):
    if not WIDE:
        return np.ones(k)
    levels = np.array([30, -30])
    if k % 512:
        return np.exp2(np.random.permutation(np.resize(levels, k // 32))).repeat(32)
    a = np.empty((k // 512, 16))
    for p in range(k // 512):
        a[p, :8] = np.random.permutation(np.resize(levels, 8))
        for g in range(8):
            far = levels[np.abs(levels - a[p, g]) >= 10]
            a[p, g + 8] = far[np.random.randint(len(far))]
    return np.exp2(a.ravel()).repeat(32)


def f64(x):
    return np.asarray(x).astype(np.float64)


def striped(idx):
    return np.tile(np.asarray(idx).reshape(-1, 16).T, (8, 1)).astype(np.uint16)


def unstriped(offs):
    return offs[:16].T.reshape(-1).astype(np.int64)


E2M1 = np.array([0.0, 0.5, 1.0, 1.5, 2.0, 3.0, 4.0, 6.0, -0.0, -0.5, -1.0, -1.5, -2.0, -3.0, -4.0, -6.0])


def pack_weight(w, fmt):
    k, n = w.shape
    w = f64(np.asarray(w, np.float32).astype(ml_dtypes.bfloat16)).reshape(k // 32, 32, n)
    amax = np.abs(w).max(1)
    if fmt in ("e4m3", "e5m2"):
        byte = np.frexp(amax)[1] - 1 + 127 - (7 if fmt == "e4m3" else 14)
    else:
        mant, ex = np.frexp(amax / 6.0)
        byte = np.where(mant > 0.5, ex, ex - 1) + 127
    byte = np.clip(np.where(amax > 0, byte, 1), 1, 254)
    scaled = (w * np.exp2(127.0 - byte)[:, None, :]).reshape(k, n).astype(np.float32)
    by_word = np.ascontiguousarray(scaled.reshape(k // 512, 128, 4, n).transpose(0, 1, 3, 2))
    if fmt in ("e4m3", "e5m2"):
        words = by_word.astype(ml_dtypes.float8_e4m3fn if fmt == "e4m3" else ml_dtypes.float8_e5m2).view(np.uint8)
    else:
        c = by_word.astype(ml_dtypes.float4_e2m1fn).view(np.uint8) & 0xF
        words = (c[..., 0::2] | (c[..., 1::2] << 4)).reshape(k // 512, 128, 2 * n)
    return np.ascontiguousarray(words), np.ascontiguousarray(byte.astype(np.uint8).reshape(k // 512, 16, n))


def unpack_weight(words, scales, fmt):
    g, _, n = scales.shape
    words = np.ascontiguousarray(words).reshape(g, 128, n, -1)
    if fmt in ("e4m3", "e5m2"):
        vals = words.view(ml_dtypes.float8_e4m3fn if fmt == "e4m3" else ml_dtypes.float8_e5m2).astype(np.float64)
    else:
        nib = np.empty((g, 128, n, 4), np.uint8)
        nib[..., 0::2] = words & 0xF
        nib[..., 1::2] = words >> 4
        vals = E2M1[nib]
    vals = vals * np.repeat(np.exp2(scales.astype(np.float64) - 127.0), 8, axis=1)[..., None]
    return vals.transpose(0, 1, 3, 2).reshape(g * 512, n)


def bf(x):
    return np.asarray(x, np.float32).astype(ml_dtypes.bfloat16)


def planes(Y):
    r, m = Y.shape
    b = f64(bf(Y)).reshape(r // 32, 32, m)
    amax = np.abs(b).max(1)
    byte = np.clip(np.where(amax > 0, np.frexp(amax)[1] - 1 + 127 - 7, 1), 1, 254)
    codes = (b * np.exp2(127.0 - byte)[:, None, :]).reshape(r, m).astype(np.float32).astype(ml_dtypes.float8_e4m3fn).view(np.uint8)
    words = codes.reshape(r // 512, 128, 4, m).transpose(0, 1, 3, 2)
    return np.ascontiguousarray(words), np.ascontiguousarray(byte.astype(np.uint8).reshape(r // 512, 16, m))


K, T, J, R, F, G, N, C = 512, 512, 256, 512, 512, 32, 512, 1024


def setup_inputs():
    n = np.random.standard_normal
    idx = np.random.permutation(T)[:J]
    idx2 = np.random.permutation(C)[:J]
    fk = mx_kscale(K)
    fr = mx_kscale(R)
    ff = mx_kscale(F)
    wp = pack_weight(n((K, R)) * 1 / np.sqrt(K) * fk[:, None] * fr, "e5m2")
    sxp = pack_weight(n((F, J)) / ff[:, None], "e5m2")
    w2p = pack_weight(n((F, R)) * 1 / np.sqrt(F) * ff[:, None] * fr, "e4m3")
    wbp = pack_weight(n((R, N)) * 1 / np.sqrt(R) / fr[:, None], "e2m1")
    return {
        "xf": (n((K, T))).astype(np.float32),
        "ow": (n((K, J)) * 0.7).astype(np.float32),
        "fk": (np.random.uniform(0.5, 2.0, (K, 1)) / fk[:, None]).astype(np.float32),
        "w_words": wp[0],
        "w_scales": wp[1],
        "sx_words": sxp[0],
        "sx_scales": sxp[1],
        "w2_words": w2p[0],
        "w2_scales": w2p[1],
        "wb_words": wbp[0],
        "wb_scales": wbp[1],
        "old": (1.0 * n((N, C))).astype(np.float32),
        "offs": striped(idx),
        "offs2": striped(idx2),
    }


def reference(xf, ow, fk, w_words, w_scales, sx_words, sx_scales, w2_words, w2_scales, wb_words, wb_scales, old, offs, offs2):
    idx = unstriped(offs)
    idx2 = unstriped(offs2)
    wu = unpack_weight(w_words, w_scales, "e5m2")
    sxu = unpack_weight(sx_words, sx_scales, "e5m2")
    w2u = unpack_weight(w2_words, w2_scales, "e4m3")
    wbu = unpack_weight(wb_words, wb_scales, "e2m1")
    u = (f64(xf)[:, idx] - f64(ow)) * f64(fk)
    uq = mxq(u, 0, "e5m2")
    a = wu.T @ uq + w2u.T @ sxu
    m1 = a.reshape(R, G, J // G).mean(axis=2)
    m2 = np.repeat(m1, J // G, axis=1)
    hid = a - m2
    hidq = mxq(hid, 0, "e5m2")
    p = wbu.T @ hidq
    pp = np.zeros((N, C))
    pp[:, idx2] = p
    y = pp + 0.5 * f64(old)
    words, scales = planes(y)
    return y, words, scales

@@ -1,0 +1,233 @@
+from contextlib import ExitStack
+
+import concourse.mybir as mybir
+
+K, T, J, R, N, C = 512, 512, 256, 512, 512, 1024
+FLOPS = 2 * J * (K * R + K * R + R * N)
+
+F32, BF16 = mybir.dt.float32, mybir.dt.bfloat16
+I32, U32, U16, U8 = mybir.dt.int32, mybir.dt.uint32, mybir.dt.uint16, mybir.dt.uint8
+E4M3, E5M2, E2M1 = mybir.dt.float8_e4m3fn_x4, mybir.dt.float8_e5m2_x4, mybir.dt.float4_e2m1fn_x4
+ALU = mybir.AluOpType
+COPY = mybir.ActivationFunctionType.Copy
+
+P = 128
+PACK = 4
+HALF = J // 2
+BUNDLE = 8
+CHUNK = 256
+
+
+def tile_list_sum_offsetpicks_own_levelled_scattered_pl_kernel(
+    tc, xf, ow, fk, w_words, w_scales, sx_words, sx_scales, w2_words, w2_scales, wb_words, wb_scales, old, offs, offs2,
+    out_0, out_1, out_2,
+):
+    nc = tc.nc
+    with ExitStack() as ctx:
+        pool = ctx.enter_context(tc.tile_pool(name="sb", bufs=1))
+        psum = ctx.enter_context(tc.psum_pool(name="ps", bufs=1))
+
+        def sb(name, shape, dtype):
+            return pool.tile(shape, dtype, name=name, align_bytes=64)
+
+        def words_of(dram):
+            return dram[0].rearrange("p n t -> p (n t)").bitcast(I32)
+
+        xf_rows = xf.rearrange("(p t) c -> p t c", t=PACK)
+        ow_rows = ow.rearrange("(p t) c -> p t c", t=PACK)
+        old_rows = old.rearrange("(p t) c -> p t c", t=PACK)
+        out_rows = out_0.rearrange("(p t) c -> p t c", t=PACK)
+
+        W_AT, W2_AT, WB_AT, SX_AT = 0, R, 2 * R, 2 * R + N
+        raw_scales = sb("raw_scales", [P, SX_AT], U8)
+        planes = sb("planes", [P, SX_AT + J], U8)
+        for at, scales in ((W2_AT, w2_scales), (W_AT, w_scales), (WB_AT, wb_scales)):
+            nc.vector.memset(raw_scales[:, at : at + R].bitcast(U32), 0)
+            nc.scalar.dma_start(raw_scales[0:P:8, at : at + R].bitcast(I32), scales[0].bitcast(I32))
+        nc.vector.memset(planes[:, SX_AT:].bitcast(U32), 0)
+        nc.scalar.dma_start(planes[0:P:8, SX_AT:].bitcast(I32), sx_scales[0].bitcast(I32))
+
+        picks = sb("picks", [P, J // 16], U16)
+        places = sb("places", [P, J // 16], U16)
+        xf_t = [sb(f"xf{t}", [P, T], F32) for t in range(PACK)]
+        ow_t = [sb(f"ow{u}", [P, 2, J], F32) for u in range(2)]
+        fk_t = sb("fk", [P, PACK], F32)
+        w_raw, w2_raw = sb("w_raw", [P, R], U32), sb("w2_raw", [P, R], U32)
+        sx_codes = sb("sx_codes", [P, J], U32)
+        wb_raw = sb("wb_raw", [P, 2 * N], U8)
+        old_t = [sb(f"old{t}", [P, C], F32) for t in range(PACK)]
+        nc.gpsimd.dma_start(fk_t[:], fk.rearrange("(p t) o -> p (t o)", t=PACK))
+        pages = [sb(f"page{t}", [P, C], F32) for t in range(PACK)]
+        for t in range(PACK):
+            for c0 in range(0, C, 512):
+                nc.gpsimd.memset(pages[t][:, c0 : c0 + 512], 0.0)
+        nc.sync.dma_start(picks[:], offs)
+        nc.sync.dma_start(xf_t[0][:], xf_rows[:, 0, :])
+        nc.sync.dma_start(ow_t[0][:], ow_rows[:, 0:2, :])
+        nc.sync.dma_start(xf_t[1][:], xf_rows[:, 1, :])
+        nc.vector.tensor_copy(
+            planes[:, :SX_AT].rearrange("p (s t m) -> p s t m", s=3, t=PACK),
+            raw_scales[:].rearrange("p (s m t) -> p s t m", s=3, t=PACK),
+        )
+        for r in range(1, 4):
+            nc.sync.dma_start(planes[r:P:32, :].bitcast(I32), planes[8 * r : P : 32, :].bitcast(I32))
+        nc.sync.dma_start(w2_raw[:].bitcast(I32), words_of(w2_words))
+        nc.sync.dma_start(sx_codes[:].bitcast(I32), words_of(sx_words))
+        nc.sync.dma_start(xf_t[2][:], xf_rows[:, 2, :])
+        nc.sync.dma_start(ow_t[1][:], ow_rows[:, 2:4, :])
+        nc.sync.dma_start(xf_t[3][:], xf_rows[:, 3, :])
+        nc.sync.dma_start(w_raw[:].bitcast(I32), words_of(w_words))
+        nc.sync.dma_start(wb_raw[:].bitcast(I32), wb_words[0].bitcast(I32))
+        nc.sync.dma_start(places[:], offs2)
+        for t in range(PACK):
+            nc.sync.dma_start(old_t[t][:], old_rows[:, t, :])
+
+
+        def dealt(ap):
+            return ap.rearrange("p (t b i) -> p b t i", t=PACK, i=4)
+
+        def as_given(ap):
+            return ap.rearrange("p (b i t) -> p b t i", t=PACK, i=4)
+
+        diff = sb("diff", [P, PACK, J], F32)
+        u_bf = [sb(f"u_bf{h}", [P, HALF, PACK], BF16) for h in range(2)]
+        u_codes = [sb(f"u_codes{h}", [P, HALF], U32) for h in range(2)]
+        u_scales = [sb(f"u_scales{h}", [P, HALF], U8) for h in range(2)]
+        w_codes, w2_codes = sb("w_codes", [P, R], U32), sb("w2_codes", [P, R], U32)
+        wb_codes = sb("wb_codes", [P, 2 * N], U8)
+        halves = [slice(h * HALF, (h + 1) * HALF) for h in range(2)]
+        list_halves = [slice(h * HALF // 16, (h + 1) * HALF // 16) for h in range(2)]
+
+        def scale_round(t, h):
+            nc.scalar.activation(u_bf[h][:, :, t], diff[:, t, halves[h]], COPY, scale=fk_t[:, t : t + 1])
+
+        for t in range(PACK - 1):
+            nc.vector.tensor_tensor(diff[:, t, :], xf_t[t][:].indirect(picks[:]), ow_t[t // 2][:, t % 2, :], ALU.subtract)
+            for h in range(2):
+                scale_round(t, h)
+            if t == 1:
+                nc.scalar.copy(dealt(w2_codes[:]), as_given(w2_raw[:]))
+        t = PACK - 1
+        for h in range(2):
+            nc.vector.tensor_tensor(
+                diff[:, t, halves[h]], xf_t[t][:].indirect(picks[:, list_halves[h]]), ow_t[1][:, 1, halves[h]], ALU.subtract
+            )
+            scale_round(t, h)
+        nc.vector.tensor_copy(dealt(w_codes[:].bitcast(I32)), as_given(w_raw[:].bitcast(I32)))
+
+        a_ps = [psum.tile([P, PACK, HALF], F32, name=f"a_ps{h}") for h in range(2)]
+        p_ps = [psum.tile([P, PACK, HALF], F32, name=f"p_ps{h}") for h in range(2)]
+        for h in range(2):
+            nc.vector.quantize_mx(u_codes[h][:].bitcast(E5M2), u_scales[h][:], u_bf[h][:].rearrange("p j t -> p (j t)"))
+            for t in range(PACK):
+                nc.tensor.matmul_mx(
+                    out=a_ps[h][:, t, :],
+                    lhsT=w2_codes[:, t * P : (t + 1) * P].bitcast(E4M3),
+                    lhsT_scale=planes[:, W2_AT + t * P : W2_AT + (t + 1) * P],
+                    rhs=sx_codes[:, halves[h]].bitcast(E5M2),
+                    rhs_scale=planes[:, SX_AT + h * HALF : SX_AT + (h + 1) * HALF],
+                    start=(t == 0),
+                    stop=False,
+                )
+            for t in range(PACK):
+                nc.tensor.matmul_mx(
+                    out=a_ps[h][:, t, :],
+                    lhsT=w_codes[:, t * P : (t + 1) * P].bitcast(E5M2),
+                    lhsT_scale=planes[:, W_AT + t * P : W_AT + (t + 1) * P],
+                    rhs=u_codes[h][:].bitcast(E5M2),
+                    rhs_scale=u_scales[h][:],
+                    start=False,
+                    stop=(t == PACK - 1),
+                )
+        nc.scalar.copy(dealt(wb_codes[:].bitcast(U16)), as_given(wb_raw[:].bitcast(U16)))
+
+        GH = HALF // BUNDLE
+        sums = [sb(f"sums{h}", [P, GH, PACK], F32) for h in range(2)]
+        means = [sb(f"means{h}", [P, GH, PACK], F32) for h in range(2)]
+        hid_bf = [sb(f"hid_bf{h}", [P, HALF, PACK], BF16) for h in range(2)]
+        hid_codes = [sb(f"hid_codes{h}", [P, HALF], U32) for h in range(2)]
+        hid_scales = [sb(f"hid_scales{h}", [P, HALF], U8) for h in range(2)]
+        p_sb = [sb(f"p_sb{h}", [P, PACK, HALF], F32) for h in range(2)]
+
+        def level(h):
+            a_bundles = a_ps[h][:].rearrange("p t (g i) -> p g t i", i=BUNDLE)
+            nc.vector.tensor_reduce(sums[h][:], a_bundles, mybir.AxisListType.X, ALU.add)
+            nc.vector.tensor_scalar(means[h][:], sums[h][:], 1.0 / BUNDLE, None, ALU.mult)
+            nc.vector.tensor_tensor(
+                hid_bf[h][:].rearrange("p (g i) t -> p g i t", i=BUNDLE),
+                a_ps[h][:].rearrange("p t (g i) -> p g i t", i=BUNDLE),
+                means[h][:].unsqueeze(2).to_broadcast([P, GH, BUNDLE, PACK]),
+                ALU.subtract,
+            )
+
+        def second(h):
+            nc.vector.quantize_mx(hid_codes[h][:].bitcast(E5M2), hid_scales[h][:], hid_bf[h][:].rearrange("p j t -> p (j t)"))
+            for t in range(PACK):
+                nc.tensor.matmul_mx(
+                    out=p_ps[h][:, t, :],
+                    lhsT=wb_codes[:, 2 * t * P : 2 * (t + 1) * P].bitcast(E2M1),
+                    lhsT_scale=planes[:, WB_AT + t * P : WB_AT + (t + 1) * P],
+                    rhs=hid_codes[h][:].bitcast(E5M2),
+                    rhs_scale=hid_scales[h][:],
+                    start=True,
+                    stop=True,
+                )
+
+        level(0)
+        second(0)
+        level(1)
+        second(1)
+        nc.scalar.copy(p_sb[0][:], p_ps[0][:])
+        nc.vector.tensor_copy(p_sb[1][:], p_ps[1][:])
+
+        y = sb("y", [P, PACK, C], F32)
+        y_bf = [sb(f"y_bf{q}", [P, CHUNK, PACK], BF16) for q in range(C // CHUNK)]
+        y_codes = sb("y_codes", [P, C], U32)
+        y_scales = sb("y_scales", [P, C], U8)
+
+        def put_scalar(t, h):
+            nc.scalar.activation(pages[t][:].indirect(places[:, list_halves[h]]), p_sb[h][:, t, :], COPY)
+
+        def add_old(t, cols):
+            nc.vector.scalar_tensor_tensor(y[:, t, cols], old_t[t][:, cols], 0.5, pages[t][:, cols], ALU.mult, ALU.add)
+
+        put_scalar(0, 0)
+        nc.vector.tensor_copy(pages[0][:].indirect(places[:, list_halves[1]]), p_sb[1][:, 0, :])
+        for t in range(PACK):
+            if t > 0:
+                put_scalar(t, 0)
+                put_scalar(t, 1)
+            if t < PACK - 1:
+                add_old(t, slice(0, C))
+                nc.sync.dma_start(out_rows[:, t, :], y[:, t, :])
+        chunks = [slice(q * CHUNK, (q + 1) * CHUNK) for q in range(C // CHUNK)]
+        for q, cols in enumerate(chunks):
+            add_old(PACK - 1, cols)
+            if q % 2 == 1:
+                both = slice((q - 1) * CHUNK, (q + 1) * CHUNK)
+                nc.sync.dma_start(out_rows[:, PACK - 1, both], y[:, PACK - 1, both])
+
+        def weave(q, copy):
+            copy(
+                y_bf[q][:].rearrange("p (b i) t -> p b t i", i=4),
+                y[:, :, chunks[q]].rearrange("p t (b i) -> p b t i", i=4),
+            )
+
+        out_words = words_of(out_1)
+
+        def pack(q):
+            nc.vector.quantize_mx(
+                y_codes[:, chunks[q]].bitcast(E4M3), y_scales[:, chunks[q]], y_bf[q][:].rearrange("p c t -> p (c t)")
+            )
+            nc.sync.dma_start(out_words[:, chunks[q]], y_codes[:, chunks[q]].bitcast(I32))
+
+        weave(0, nc.scalar.copy)
+        weave(1, nc.scalar.copy)
+        weave(2, nc.vector.tensor_copy)
+        weave(3, nc.vector.tensor_copy)
+        for q in (0, 2, 3, 1):
+            pack(q)
+        out_scale_rows = out_2[0].bitcast(I32)
+        for r in range(4):
+            queue = nc.sync if r % 2 == 0 else nc.scalar
+            queue.dma_start(out_scale_rows[r:16:4, :], y_scales[r:P:32, :].bitcast(I32))

@@ -25,6 +25,7 @@ def tile_list_sum_offsetpicks_own_levelled_scattered_pl_kernel(
     nc = tc.nc
     with ExitStack() as ctx:
         pool = ctx.enter_context(tc.tile_pool(name="sb", bufs=1))
+        shared = ctx.enter_context(tc.tile_pool(name="shared", bufs=1))
         psum = ctx.enter_context(tc.psum_pool(name="ps", bufs=1))
 
         def sb(name, shape, dtype):
@@ -39,48 +40,51 @@ def tile_list_sum_offsetpicks_own_levelled_scattered_pl_kernel(
         out_rows = out_0.rearrange("(p t) c -> p t c", t=PACK)
 
         W_AT, W2_AT, WB_AT, SX_AT = 0, R, 2 * R, 2 * R + N
-        raw_scales = sb("raw_scales", [P, SX_AT], U8)
+        raw_scales = shared.tile([P, SX_AT], U8, name="raw_scales", offset=4 * R - 64)
         planes = sb("planes", [P, SX_AT + J], U8)
-        for at, scales in ((W2_AT, w2_scales), (W_AT, w_scales), (WB_AT, wb_scales)):
+        for at in (W_AT, WB_AT, W2_AT):
             nc.vector.memset(raw_scales[:, at : at + R].bitcast(U32), 0)
-            nc.scalar.dma_start(raw_scales[0:P:8, at : at + R].bitcast(I32), scales[0].bitcast(I32))
         nc.vector.memset(planes[:, SX_AT:].bitcast(U32), 0)
-        nc.scalar.dma_start(planes[0:P:8, SX_AT:].bitcast(I32), sx_scales[0].bitcast(I32))
+        for queue, at, scales in ((nc.scalar, W_AT, w_scales), (nc.sync, WB_AT, wb_scales), (nc.scalar, W2_AT, w2_scales)):
+            queue.dma_start(raw_scales[0:P:8, at : at + R].bitcast(I32), scales[0].bitcast(I32))
+        nc.sync.dma_start(planes[0:P:8, SX_AT:].bitcast(I32), sx_scales[0].bitcast(I32))
 
         picks = sb("picks", [P, J // 16], U16)
         places = sb("places", [P, J // 16], U16)
         xf_t = [sb(f"xf{t}", [P, T], F32) for t in range(PACK)]
         ow_t = [sb(f"ow{u}", [P, 2, J], F32) for u in range(2)]
-        fk_t = sb("fk", [P, PACK], F32)
-        w_raw, w2_raw = sb("w_raw", [P, R], U32), sb("w2_raw", [P, R], U32)
+        fk_landed, fk_t = sb("fk_landed", [P, PACK], F32), sb("fk", [P, PACK], F32)
+        w_raw = shared.tile([P, R], U32, name="w_raw", offset=0)
+        w2_raw = sb("w2_raw", [P, R], U32)
         sx_codes = sb("sx_codes", [P, J], U32)
-        wb_raw = sb("wb_raw", [P, 2 * N], U8)
-        old_t = [sb(f"old{t}", [P, C], F32) for t in range(PACK)]
-        nc.gpsimd.dma_start(fk_t[:], fk.rearrange("(p t) o -> p (t o)", t=PACK))
-        pages = [sb(f"page{t}", [P, C], F32) for t in range(PACK)]
-        for t in range(PACK):
-            for c0 in range(0, C, 512):
-                nc.gpsimd.memset(pages[t][:, c0 : c0 + 512], 0.0)
+        wb_raw = shared.tile([P, 2 * N], U8, name="wb_raw", offset=4 * R)
+        old_t = shared.tile([P, PACK, C], F32, name="old", offset=4 * R + SX_AT - 128)
+        nc.scalar.dma_start(fk_landed[:], fk.rearrange("(p t) o -> p (t o)", t=PACK))
+        pages = [sb(f"page{t}", [P, C], F32) for t in range(PACK - 1)]
+        for page in pages:
+            nc.vector.memset(page[:], 0.0)
         nc.sync.dma_start(picks[:], offs)
         nc.sync.dma_start(xf_t[0][:], xf_rows[:, 0, :])
         nc.sync.dma_start(ow_t[0][:], ow_rows[:, 0:2, :])
         nc.sync.dma_start(xf_t[1][:], xf_rows[:, 1, :])
-        nc.vector.tensor_copy(
-            planes[:, :SX_AT].rearrange("p (s t m) -> p s t m", s=3, t=PACK),
-            raw_scales[:].rearrange("p (s m t) -> p s t m", s=3, t=PACK),
-        )
+        nc.sync.dma_start(ow_t[1][:], ow_rows[:, 2:4, :])
+        nc.sync.dma_start(xf_t[2][:], xf_rows[:, 2, :])
+        nc.vector.tensor_copy(fk_t[:], fk_landed[:])
+        for first, end in ((W_AT, WB_AT), (WB_AT, SX_AT)):
+            nc.vector.tensor_copy(
+                planes[:, first:end].rearrange("p (s t m) -> p s t m", t=PACK, m=P),
+                raw_scales[:, first:end].rearrange("p (s m t) -> p s t m", t=PACK, m=P),
+            )
         for r in range(1, 4):
             nc.sync.dma_start(planes[r:P:32, :].bitcast(I32), planes[8 * r : P : 32, :].bitcast(I32))
         nc.sync.dma_start(w2_raw[:].bitcast(I32), words_of(w2_words))
         nc.sync.dma_start(sx_codes[:].bitcast(I32), words_of(sx_words))
-        nc.sync.dma_start(xf_t[2][:], xf_rows[:, 2, :])
-        nc.sync.dma_start(ow_t[1][:], ow_rows[:, 2:4, :])
         nc.sync.dma_start(xf_t[3][:], xf_rows[:, 3, :])
         nc.sync.dma_start(w_raw[:].bitcast(I32), words_of(w_words))
         nc.sync.dma_start(wb_raw[:].bitcast(I32), wb_words[0].bitcast(I32))
         nc.sync.dma_start(places[:], offs2)
         for t in range(PACK):
-            nc.sync.dma_start(old_t[t][:], old_rows[:, t, :])
+            nc.sync.dma_start(old_t[:, t, :], old_rows[:, t, :])
 
 
         def dealt(ap):
@@ -89,7 +93,7 @@ def tile_list_sum_offsetpicks_own_levelled_scattered_pl_kernel(
         def as_given(ap):
             return ap.rearrange("p (b i t) -> p b t i", t=PACK, i=4)
 
-        diff = sb("diff", [P, PACK, J], F32)
+        diff = pool.tile([P, PACK, J], F32, name="diff", tag="diff_then_page", align_bytes=64)
         u_bf = [sb(f"u_bf{h}", [P, HALF, PACK], BF16) for h in range(2)]
         u_codes = [sb(f"u_codes{h}", [P, HALF], U32) for h in range(2)]
         u_scales = [sb(f"u_scales{h}", [P, HALF], U8) for h in range(2)]
@@ -105,8 +109,7 @@ def tile_list_sum_offsetpicks_own_levelled_scattered_pl_kernel(
             nc.vector.tensor_tensor(diff[:, t, :], xf_t[t][:].indirect(picks[:]), ow_t[t // 2][:, t % 2, :], ALU.subtract)
             for h in range(2):
                 scale_round(t, h)
-            if t == 1:
-                nc.scalar.copy(dealt(w2_codes[:]), as_given(w2_raw[:]))
+        nc.vector.tensor_copy(dealt(w2_codes[:].bitcast(I32)), as_given(w2_raw[:].bitcast(I32)))
         t = PACK - 1
         for h in range(2):
             nc.vector.tensor_tensor(
@@ -118,7 +121,6 @@ def tile_list_sum_offsetpicks_own_levelled_scattered_pl_kernel(
         a_ps = [psum.tile([P, PACK, HALF], F32, name=f"a_ps{h}") for h in range(2)]
         p_ps = [psum.tile([P, PACK, HALF], F32, name=f"p_ps{h}") for h in range(2)]
         for h in range(2):
-            nc.vector.quantize_mx(u_codes[h][:].bitcast(E5M2), u_scales[h][:], u_bf[h][:].rearrange("p j t -> p (j t)"))
             for t in range(PACK):
                 nc.tensor.matmul_mx(
                     out=a_ps[h][:, t, :],
@@ -129,6 +131,8 @@ def tile_list_sum_offsetpicks_own_levelled_scattered_pl_kernel(
                     start=(t == 0),
                     stop=False,
                 )
+        for h in range(2):
+            nc.vector.quantize_mx(u_codes[h][:].bitcast(E5M2), u_scales[h][:], u_bf[h][:].rearrange("p j t -> p (j t)"))
             for t in range(PACK):
                 nc.tensor.matmul_mx(
                     out=a_ps[h][:, t, :],
@@ -139,6 +143,8 @@ def tile_list_sum_offsetpicks_own_levelled_scattered_pl_kernel(
                     start=False,
                     stop=(t == PACK - 1),
                 )
+        pages.append(pool.tile([P, C], F32, name="page3", tag="diff_then_page", align_bytes=64))
+        nc.vector.memset(pages[PACK - 1][:], 0.0)
         nc.scalar.copy(dealt(wb_codes[:].bitcast(U16)), as_given(wb_raw[:].bitcast(U16)))
 
         GH = HALF // BUNDLE
@@ -149,10 +155,12 @@ def tile_list_sum_offsetpicks_own_levelled_scattered_pl_kernel(
         hid_scales = [sb(f"hid_scales{h}", [P, HALF], U8) for h in range(2)]
         p_sb = [sb(f"p_sb{h}", [P, PACK, HALF], F32) for h in range(2)]
 
-        def level(h):
+        def bundle_means(h):
             a_bundles = a_ps[h][:].rearrange("p t (g i) -> p g t i", i=BUNDLE)
             nc.vector.tensor_reduce(sums[h][:], a_bundles, mybir.AxisListType.X, ALU.add)
-            nc.vector.tensor_scalar(means[h][:], sums[h][:], 1.0 / BUNDLE, None, ALU.mult)
+            nc.scalar.activation(means[h][:], sums[h][:], COPY, scale=1.0 / BUNDLE)
+
+        def level(h):
             nc.vector.tensor_tensor(
                 hid_bf[h][:].rearrange("p (g i) t -> p g i t", i=BUNDLE),
                 a_ps[h][:].rearrange("p t (g i) -> p g i t", i=BUNDLE),
@@ -173,60 +181,49 @@ def tile_list_sum_offsetpicks_own_levelled_scattered_pl_kernel(
                     stop=True,
                 )
 
-        level(0)
-        second(0)
-        level(1)
-        second(1)
+        for step in (bundle_means, level, second):
+            for h in range(2):
+                step(h)
         nc.scalar.copy(p_sb[0][:], p_ps[0][:])
         nc.vector.tensor_copy(p_sb[1][:], p_ps[1][:])
 
+        edges = (0, 128, 512, 640, C)
+        chunks = [slice(a, b) for a, b in zip(edges, edges[1:])]
         y = sb("y", [P, PACK, C], F32)
-        y_bf = [sb(f"y_bf{q}", [P, CHUNK, PACK], BF16) for q in range(C // CHUNK)]
+        y_bf = [sb(f"y_bf{q}", [P, cols.stop - cols.start, PACK], BF16) for q, cols in enumerate(chunks)]
         y_codes = sb("y_codes", [P, C], U32)
         y_scales = sb("y_scales", [P, C], U8)
 
-        def put_scalar(t, h):
-            nc.scalar.activation(pages[t][:].indirect(places[:, list_halves[h]]), p_sb[h][:, t, :], COPY)
-
         def add_old(t, cols):
-            nc.vector.scalar_tensor_tensor(y[:, t, cols], old_t[t][:, cols], 0.5, pages[t][:, cols], ALU.mult, ALU.add)
+            nc.vector.scalar_tensor_tensor(y[:, t, cols], old_t[:, t, cols], 0.5, pages[t][:, cols], ALU.mult, ALU.add)
 
-        put_scalar(0, 0)
-        nc.vector.tensor_copy(pages[0][:].indirect(places[:, list_halves[1]]), p_sb[1][:, 0, :])
         for t in range(PACK):
-            if t > 0:
-                put_scalar(t, 0)
-                put_scalar(t, 1)
+            for h in range(2):
+                listed = pages[t][:].indirect(places[:, list_halves[h]])
+                if t == 0:
+                    nc.vector.tensor_copy(listed, p_sb[h][:, t, :])
+                else:
+                    nc.scalar.activation(listed, p_sb[h][:, t, :], COPY)
             if t < PACK - 1:
                 add_old(t, slice(0, C))
                 nc.sync.dma_start(out_rows[:, t, :], y[:, t, :])
-        chunks = [slice(q * CHUNK, (q + 1) * CHUNK) for q in range(C // CHUNK)]
         for q, cols in enumerate(chunks):
             add_old(PACK - 1, cols)
             if q % 2 == 1:
-                both = slice((q - 1) * CHUNK, (q + 1) * CHUNK)
+                both = slice(chunks[q - 1].start, cols.stop)
                 nc.sync.dma_start(out_rows[:, PACK - 1, both], y[:, PACK - 1, both])
 
-        def weave(q, copy):
+        for q, cols in enumerate(chunks):
+            copy = nc.scalar.copy if q < 3 else nc.vector.tensor_copy
             copy(
                 y_bf[q][:].rearrange("p (b i) t -> p b t i", i=4),
-                y[:, :, chunks[q]].rearrange("p t (b i) -> p b t i", i=4),
+                y[:, :, cols].rearrange("p t (b i) -> p b t i", i=4),
             )
-
         out_words = words_of(out_1)
-
-        def pack(q):
-            nc.vector.quantize_mx(
-                y_codes[:, chunks[q]].bitcast(E4M3), y_scales[:, chunks[q]], y_bf[q][:].rearrange("p c t -> p (c t)")
-            )
-            nc.sync.dma_start(out_words[:, chunks[q]], y_codes[:, chunks[q]].bitcast(I32))
-
-        weave(0, nc.scalar.copy)
-        weave(1, nc.scalar.copy)
-        weave(2, nc.vector.tensor_copy)
-        weave(3, nc.vector.tensor_copy)
-        for q in (0, 2, 3, 1):
-            pack(q)
+        for q in (0, 3, 1, 2):
+            cols = chunks[q]
+            nc.vector.quantize_mx(y_codes[:, cols].bitcast(E4M3), y_scales[:, cols], y_bf[q][:].rearrange("p c t -> p (c t)"))
+            nc.sync.dma_start(out_words[:, cols], y_codes[:, cols].bitcast(I32))
         out_scale_rows = out_2[0].bitcast(I32)
         for r in range(4):
             queue = nc.sync if r % 2 == 0 else nc.scalar

from contextlib import ExitStack

import concourse.mybir as mybir

K, T, J, R, N, C = 512, 512, 256, 512, 512, 1024
FLOPS = 2 * J * (K * R + K * R + R * N)

F32, BF16 = mybir.dt.float32, mybir.dt.bfloat16
I32, U32, U16, U8 = mybir.dt.int32, mybir.dt.uint32, mybir.dt.uint16, mybir.dt.uint8
E4M3, E5M2, E2M1 = mybir.dt.float8_e4m3fn_x4, mybir.dt.float8_e5m2_x4, mybir.dt.float4_e2m1fn_x4
ALU = mybir.AluOpType
COPY = mybir.ActivationFunctionType.Copy

P = 128
PACK = 4
HALF = J // 2
BUNDLE = 8
CHUNK = 256


def tile_list_sum_offsetpicks_own_levelled_scattered_pl_kernel(
    tc, xf, ow, fk, w_words, w_scales, sx_words, sx_scales, w2_words, w2_scales, wb_words, wb_scales, old, offs, offs2,
    out_0, out_1, out_2,
):
    nc = tc.nc
    with ExitStack() as ctx:
        pool = ctx.enter_context(tc.tile_pool(name="sb", bufs=1))
        shared = ctx.enter_context(tc.tile_pool(name="shared", bufs=1))
        psum = ctx.enter_context(tc.psum_pool(name="ps", bufs=1))

        def sb(name, shape, dtype):
            return pool.tile(shape, dtype, name=name, align_bytes=64)

        def words_of(dram):
            return dram[0].rearrange("p n t -> p (n t)").bitcast(I32)

        xf_rows = xf.rearrange("(p t) c -> p t c", t=PACK)
        ow_rows = ow.rearrange("(p t) c -> p t c", t=PACK)
        old_rows = old.rearrange("(p t) c -> p t c", t=PACK)
        out_rows = out_0.rearrange("(p t) c -> p t c", t=PACK)

        W_AT, W2_AT, WB_AT, SX_AT = 0, R, 2 * R, 2 * R + N
        raw_scales = shared.tile([P, SX_AT], U8, name="raw_scales", offset=4 * R - 64)
        planes = sb("planes", [P, SX_AT + J], U8)
        for at in (W_AT, WB_AT, W2_AT):
            nc.vector.memset(raw_scales[:, at : at + R].bitcast(U32), 0)
        nc.vector.memset(planes[:, SX_AT:].bitcast(U32), 0)
        for queue, at, scales in ((nc.scalar, W_AT, w_scales), (nc.sync, WB_AT, wb_scales), (nc.scalar, W2_AT, w2_scales)):
            queue.dma_start(raw_scales[0:P:8, at : at + R].bitcast(I32), scales[0].bitcast(I32))
        nc.sync.dma_start(planes[0:P:8, SX_AT:].bitcast(I32), sx_scales[0].bitcast(I32))

        picks = sb("picks", [P, J // 16], U16)
        places = sb("places", [P, J // 16], U16)
        xf_t = [sb(f"xf{t}", [P, T], F32) for t in range(PACK)]
        ow_t = [sb(f"ow{u}", [P, 2, J], F32) for u in range(2)]
        fk_landed, fk_t = sb("fk_landed", [P, PACK], F32), sb("fk", [P, PACK], F32)
        w_raw = shared.tile([P, R], U32, name="w_raw", offset=0)
        w2_raw = sb("w2_raw", [P, R], U32)
        sx_codes = sb("sx_codes", [P, J], U32)
        wb_raw = shared.tile([P, 2 * N], U8, name="wb_raw", offset=4 * R)
        old_t = shared.tile([P, PACK, C], F32, name="old", offset=4 * R + SX_AT - 128)
        nc.scalar.dma_start(fk_landed[:], fk.rearrange("(p t) o -> p (t o)", t=PACK))
        pages = [sb(f"page{t}", [P, C], F32) for t in range(PACK - 1)]
        for page in pages:
            nc.vector.memset(page[:], 0.0)
        nc.sync.dma_start(picks[:], offs)
        nc.sync.dma_start(xf_t[0][:], xf_rows[:, 0, :])
        nc.sync.dma_start(ow_t[0][:], ow_rows[:, 0:2, :])
        nc.sync.dma_start(xf_t[1][:], xf_rows[:, 1, :])
        nc.sync.dma_start(ow_t[1][:], ow_rows[:, 2:4, :])
        nc.sync.dma_start(xf_t[2][:], xf_rows[:, 2, :])
        nc.vector.tensor_copy(fk_t[:], fk_landed[:])
        for first, end in ((W_AT, WB_AT), (WB_AT, SX_AT)):
            nc.vector.tensor_copy(
                planes[:, first:end].rearrange("p (s t m) -> p s t m", t=PACK, m=P),
                raw_scales[:, first:end].rearrange("p (s m t) -> p s t m", t=PACK, m=P),
            )
        for r in range(1, 4):
            nc.sync.dma_start(planes[r:P:32, :].bitcast(I32), planes[8 * r : P : 32, :].bitcast(I32))
        nc.sync.dma_start(w2_raw[:].bitcast(I32), words_of(w2_words))
        nc.sync.dma_start(sx_codes[:].bitcast(I32), words_of(sx_words))
        nc.sync.dma_start(xf_t[3][:], xf_rows[:, 3, :])
        nc.sync.dma_start(w_raw[:].bitcast(I32), words_of(w_words))
        nc.sync.dma_start(wb_raw[:].bitcast(I32), wb_words[0].bitcast(I32))
        nc.sync.dma_start(places[:], offs2)
        for t in range(PACK):
            nc.sync.dma_start(old_t[:, t, :], old_rows[:, t, :])


        def dealt(ap):
            return ap.rearrange("p (t b i) -> p b t i", t=PACK, i=4)

        def as_given(ap):
            return ap.rearrange("p (b i t) -> p b t i", t=PACK, i=4)

        diff = pool.tile([P, PACK, J], F32, name="diff", tag="diff_then_page", align_bytes=64)
        u_bf = [sb(f"u_bf{h}", [P, HALF, PACK], BF16) for h in range(2)]
        u_codes = [sb(f"u_codes{h}", [P, HALF], U32) for h in range(2)]
        u_scales = [sb(f"u_scales{h}", [P, HALF], U8) for h in range(2)]
        w_codes, w2_codes = sb("w_codes", [P, R], U32), sb("w2_codes", [P, R], U32)
        wb_codes = sb("wb_codes", [P, 2 * N], U8)
        halves = [slice(h * HALF, (h + 1) * HALF) for h in range(2)]
        list_halves = [slice(h * HALF // 16, (h + 1) * HALF // 16) for h in range(2)]

        def scale_round(t, h):
            nc.scalar.activation(u_bf[h][:, :, t], diff[:, t, halves[h]], COPY, scale=fk_t[:, t : t + 1])

        for t in range(PACK - 1):
            nc.vector.tensor_tensor(diff[:, t, :], xf_t[t][:].indirect(picks[:]), ow_t[t // 2][:, t % 2, :], ALU.subtract)
            for h in range(2):
                scale_round(t, h)
        nc.vector.tensor_copy(dealt(w2_codes[:].bitcast(I32)), as_given(w2_raw[:].bitcast(I32)))
        t = PACK - 1
        for h in range(2):
            nc.vector.tensor_tensor(
                diff[:, t, halves[h]], xf_t[t][:].indirect(picks[:, list_halves[h]]), ow_t[1][:, 1, halves[h]], ALU.subtract
            )
            scale_round(t, h)
        nc.vector.tensor_copy(dealt(w_codes[:].bitcast(I32)), as_given(w_raw[:].bitcast(I32)))

        a_ps = [psum.tile([P, PACK, HALF], F32, name=f"a_ps{h}") for h in range(2)]
        p_ps = [psum.tile([P, PACK, HALF], F32, name=f"p_ps{h}") for h in range(2)]
        for h in range(2):
            for t in range(PACK):
                nc.tensor.matmul_mx(
                    out=a_ps[h][:, t, :],
                    lhsT=w2_codes[:, t * P : (t + 1) * P].bitcast(E4M3),
                    lhsT_scale=planes[:, W2_AT + t * P : W2_AT + (t + 1) * P],
                    rhs=sx_codes[:, halves[h]].bitcast(E5M2),
                    rhs_scale=planes[:, SX_AT + h * HALF : SX_AT + (h + 1) * HALF],
                    start=(t == 0),
                    stop=False,
                )
        for h in range(2):
            nc.vector.quantize_mx(u_codes[h][:].bitcast(E5M2), u_scales[h][:], u_bf[h][:].rearrange("p j t -> p (j t)"))
            for t in range(PACK):
                nc.tensor.matmul_mx(
                    out=a_ps[h][:, t, :],
                    lhsT=w_codes[:, t * P : (t + 1) * P].bitcast(E5M2),
                    lhsT_scale=planes[:, W_AT + t * P : W_AT + (t + 1) * P],
                    rhs=u_codes[h][:].bitcast(E5M2),
                    rhs_scale=u_scales[h][:],
                    start=False,
                    stop=(t == PACK - 1),
                )
        pages.append(pool.tile([P, C], F32, name="page3", tag="diff_then_page", align_bytes=64))
        nc.vector.memset(pages[PACK - 1][:], 0.0)
        nc.scalar.copy(dealt(wb_codes[:].bitcast(U16)), as_given(wb_raw[:].bitcast(U16)))

        GH = HALF // BUNDLE
        sums = [sb(f"sums{h}", [P, GH, PACK], F32) for h in range(2)]
        means = [sb(f"means{h}", [P, GH, PACK], F32) for h in range(2)]
        hid_bf = [sb(f"hid_bf{h}", [P, HALF, PACK], BF16) for h in range(2)]
        hid_codes = [sb(f"hid_codes{h}", [P, HALF], U32) for h in range(2)]
        hid_scales = [sb(f"hid_scales{h}", [P, HALF], U8) for h in range(2)]
        p_sb = [sb(f"p_sb{h}", [P, PACK, HALF], F32) for h in range(2)]

        def bundle_means(h):
            a_bundles = a_ps[h][:].rearrange("p t (g i) -> p g t i", i=BUNDLE)
            nc.vector.tensor_reduce(sums[h][:], a_bundles, mybir.AxisListType.X, ALU.add)
            nc.scalar.activation(means[h][:], sums[h][:], COPY, scale=1.0 / BUNDLE)

        def level(h):
            nc.vector.tensor_tensor(
                hid_bf[h][:].rearrange("p (g i) t -> p g i t", i=BUNDLE),
                a_ps[h][:].rearrange("p t (g i) -> p g i t", i=BUNDLE),
                means[h][:].unsqueeze(2).to_broadcast([P, GH, BUNDLE, PACK]),
                ALU.subtract,
            )

        def second(h):
            nc.vector.quantize_mx(hid_codes[h][:].bitcast(E5M2), hid_scales[h][:], hid_bf[h][:].rearrange("p j t -> p (j t)"))
            for t in range(PACK):
                nc.tensor.matmul_mx(
                    out=p_ps[h][:, t, :],
                    lhsT=wb_codes[:, 2 * t * P : 2 * (t + 1) * P].bitcast(E2M1),
                    lhsT_scale=planes[:, WB_AT + t * P : WB_AT + (t + 1) * P],
                    rhs=hid_codes[h][:].bitcast(E5M2),
                    rhs_scale=hid_scales[h][:],
                    start=True,
                    stop=True,
                )

        for step in (bundle_means, level, second):
            for h in range(2):
                step(h)
        nc.scalar.copy(p_sb[0][:], p_ps[0][:])
        nc.vector.tensor_copy(p_sb[1][:], p_ps[1][:])

        edges = (0, 128, 512, 640, C)
        chunks = [slice(a, b) for a, b in zip(edges, edges[1:])]
        y = sb("y", [P, PACK, C], F32)
        y_bf = [sb(f"y_bf{q}", [P, cols.stop - cols.start, PACK], BF16) for q, cols in enumerate(chunks)]
        y_codes = sb("y_codes", [P, C], U32)
        y_scales = sb("y_scales", [P, C], U8)

        def add_old(t, cols):
            nc.vector.scalar_tensor_tensor(y[:, t, cols], old_t[:, t, cols], 0.5, pages[t][:, cols], ALU.mult, ALU.add)

        for t in range(PACK):
            for h in range(2):
                listed = pages[t][:].indirect(places[:, list_halves[h]])
                if t == 0:
                    nc.vector.tensor_copy(listed, p_sb[h][:, t, :])
                else:
                    nc.scalar.activation(listed, p_sb[h][:, t, :], COPY)
            if t < PACK - 1:
                add_old(t, slice(0, C))
                nc.sync.dma_start(out_rows[:, t, :], y[:, t, :])
        for q, cols in enumerate(chunks):
            add_old(PACK - 1, cols)
            if q % 2 == 1:
                both = slice(chunks[q - 1].start, cols.stop)
                nc.sync.dma_start(out_rows[:, PACK - 1, both], y[:, PACK - 1, both])

        for q, cols in enumerate(chunks):
            copy = nc.scalar.copy if q < 3 else nc.vector.tensor_copy
            copy(
                y_bf[q][:].rearrange("p (b i) t -> p b t i", i=4),
                y[:, :, cols].rearrange("p t (b i) -> p b t i", i=4),
            )
        out_words = words_of(out_1)
        for q in (0, 3, 1, 2):
            cols = chunks[q]
            nc.vector.quantize_mx(y_codes[:, cols].bitcast(E4M3), y_scales[:, cols], y_bf[q][:].rearrange("p c t -> p (c t)"))
            nc.sync.dma_start(out_words[:, cols], y_codes[:, cols].bitcast(I32))
        out_scale_rows = out_2[0].bitcast(I32)
        for r in range(4):
            queue = nc.sync if r % 2 == 0 else nc.scalar
            queue.dma_start(out_scale_rows[r:16:4, :], y_scales[r:P:32, :].bitcast(I32))
